import numpy as np
import ml_dtypes


def mxq(x, axis, fmt="e4m3"):
    dtype, down = {"e4m3": (ml_dtypes.float8_e4m3fn, 7), "e5m2": (ml_dtypes.float8_e5m2, 14)}[fmt]
    v = np.moveaxis(np.asarray(x, np.float32).astype(ml_dtypes.bfloat16).astype(np.float64), axis, -1)
    blocks = v.reshape(v.shape[:-1] + (-1, 32))
    amax = np.abs(blocks).max(-1, keepdims=True)
    byte = np.maximum(np.where(amax > 0, np.frexp(amax)[1] - 1 + 127, 0) - down, 1)
    scale = np.exp2(byte - 127.0)
    codes = (blocks / scale).astype(np.float32).astype(dtype).astype(np.float64)
    return np.moveaxis((codes * scale).reshape(v.shape), -1, axis)


WIDE = False


def mx_kscale(k):
    if not WIDE:
        return np.ones(k)
    levels = np.array([10, -10, 5, -5, 0])
    if k % 512:
        return np.exp2(np.random.permutation(np.resize(levels, k // 32))).repeat(32)
    a = np.empty((k // 512, 16))
    for p in range(k // 512):
        a[p, :8] = np.random.permutation(np.resize(levels, 8))
        for g in range(8):
            far = levels[np.abs(levels - a[p, g]) >= 10]
            a[p, g + 8] = far[np.random.randint(len(far))]
    return np.exp2(a.ravel()).repeat(32)


BF16 = ml_dtypes.bfloat16


def bf(x):
    return np.asarray(x, np.float32).astype(BF16)


def f64(x):
    return np.asarray(x).astype(np.float64)

def planes(Y):
    n, m = Y.shape
    b = f64(bf(Y)).reshape(n // 32, 32, m)
    amax = np.abs(b).max(1)
    byte = np.clip(np.where(amax > 0, np.frexp(amax)[1] - 1 + 127 - 7, 1), 1, 254)
    codes = (b * np.exp2(127.0 - byte)[:, None, :]).reshape(n, m).astype(np.float32).astype(ml_dtypes.float8_e4m3fn).view(np.uint8)
    words = codes.reshape(n // 512, 128, 4, m).transpose(0, 1, 3, 2)
    return np.ascontiguousarray(words), np.ascontiguousarray(byte.astype(np.uint8).reshape(n // 512, 16, m))


B, N, CQ, CK = 2, 512, 512, 512

EPS = 1e-6


def channel_map(q, k, temp):
    n = q.shape[1]
    gram = mxq(q, 1, "e4m3").transpose(0, 2, 1) @ mxq(k, 1, "e4m3")
    a = temp[None, :, None] * gram / np.sqrt(n)
    e = np.exp(a - a.max(axis=-1, keepdims=True))
    return e / e.sum(axis=-1, keepdims=True)


def rms_normalize(o):
    return o / np.sqrt(np.mean(o * o, axis=-1, keepdims=True) + EPS)


def setup_inputs():
    s, t = mx_kscale(N), mx_kscale(CK)
    return {
        "q": bf(np.random.standard_normal((B, N, CQ)) * s[None, :, None]),
        "k": bf(np.random.standard_normal((B, N, CK)) / s[None, :, None]),
        "v": bf(np.random.standard_normal((B, N, CK)) * 0.03 * t[None, None, :]),
        "temp": bf(1.0 + 0.1 * np.random.standard_normal(CQ)),
        "u": bf(np.random.standard_normal(CK) * 0.03 * np.sqrt(CK / CQ) / t),
        "zs": bf(np.random.standard_normal((B, CQ)) * 0.5),
        "zb": bf(np.random.standard_normal((B, CQ)) * 0.5),
    }


def core(q, k, v, temp, u, zs, zb):
    q, k, v = f64(q), f64(k), f64(v)
    temp, u, zs, zb = f64(temp), f64(u), f64(zs), f64(zb)
    c = q.shape[2]
    p = channel_map(q, k, temp)
    pu = p * u[None, None, :] * np.sqrt(c)
    o = mxq(v, 2, "e4m3") @ mxq(pu, 2, "e4m3").transpose(0, 2, 1)
    on = rms_normalize(o)
    return on * (1.0 + zs[:, None, :]) + zb[:, None, :]


def reference(q, k, v, temp, u, zs, zb):
    R_out = core(q, k, v, temp, u, zs, zb)
    words, scales = planes(np.moveaxis(R_out, 1, 0).reshape(512, -1))
    return R_out, words, scales

@@ -1,0 +1,327 @@
+import math
+from contextlib import ExitStack
+
+import concourse.mybir as mybir
+from concourse.masks import make_identity
+
+B, N, C = 2, 512, 512
+EPS = 1e-6
+FLOPS = B * 2 * (2 * N * C * C)
+
+F32 = mybir.dt.float32
+BF16 = mybir.dt.bfloat16
+I32 = mybir.dt.int32
+U32 = mybir.dt.uint32
+U8 = mybir.dt.uint8
+FP8X4 = mybir.dt.float8_e4m3fn_x4
+ALU = mybir.AluOpType
+ACT = mybir.ActivationFunctionType
+
+P = 128
+T = 4
+
+
+def tile_diffirpriorchannelattention_x1_kernel(tc, q, k, v, temp, u, zs, zb, out_0, out_1, out_2):
+    nc = tc.nc
+    with ExitStack() as ctx:
+        keep = ctx.enter_context(tc.tile_pool(name="keep", bufs=1))
+        psum = ctx.enter_context(tc.psum_pool(name="psum", bufs=6))
+        turn = ctx.enter_context(tc.psum_pool(name="turn", bufs=2))
+        ctx.enter_context(tc.manual_schedule())
+
+        def sb(shape, dtype, name):
+            return keep.tile(shape, dtype, name=name, align_bytes=64)
+
+        raw = {}
+        grouped = {}
+        codes = {}
+        scales = {}
+        for b in range(B):
+            for x in "qkv":
+                raw[x, b] = sb([P, T, C], BF16, f"raw_{x}{b}")
+            for x in "qkvp":
+                grouped[x, b] = sb([P, C, T], BF16, f"grouped_{x}{b}")
+                codes[x, b] = sb([P, C], U32, f"codes_{x}{b}")
+                scales[x, b] = sb([P, C], U8, f"scales_{x}{b}")
+            grouped["y", b] = sb([P, C, T], BF16, f"grouped_y{b}")
+        y_codes = sb([P, B, C], U32, "y_codes")
+        y_scales = sb([P, B, C], U8, "y_scales")
+        neg_a = [[sb([P, C], F32, f"neg_a{b}_{i}") for i in range(T)] for b in range(B)]
+        expo = [[sb([P, C], F32, f"expo{b}_{i}") for i in range(T)] for b in range(B)]
+        pu = [[sb([P, C], BF16, f"pu{b}_{i}") for i in range(T)] for b in range(B)]
+        mod = [sb([P, T, C], F32, f"mod{b}") for b in range(B)]
+        res = [sb([P, T, C], F32, f"res{b}") for b in range(B)]
+        neg_max = [[sb([P, 1], F32, f"neg_max{b}_{i}") for i in range(T)] for b in range(B)]
+        total = [[sb([P, 2], F32, f"total{b}_{h}") for h in range(2)] for b in range(B)]
+        inv_total = [[sb([P, 2], F32, f"inv_total{b}_{h}") for h in range(2)] for b in range(B)]
+        ms = [[sb([P, 1], F32, f"ms{b}_{t}") for t in range(T)] for b in range(B)]
+        ms_eps = [[sb([P, 1], F32, f"ms_eps{b}_{t}") for t in range(T)] for b in range(B)]
+        rstd = [[sb([P, 1], F32, f"rstd{b}_{t}") for t in range(T)] for b in range(B)]
+        junk = sb([P, C], F32, "junk")
+        warm = sb([P, 1], F32, "warm")
+        ident = sb([P, P], F32, "ident")
+        minus_half = sb([P, 1], F32, "minus_half")
+        temp_raw = sb([P, T, 2], BF16, "temp_raw")
+        neg_temp = sb([P, T, 1], F32, "neg_temp")
+        u_raw = sb([P, C], BF16, "u_raw")
+        u_perm = sb([P, C], F32, "u_perm")
+        zs_all = sb([P, B, C], BF16, "zs_all")
+        zb_all = sb([P, B, C], BF16, "zb_all")
+
+        def load(x, src, b):
+            if x == "v":
+                nc.sync.dma_start(out=raw[x, b][:], in_=src[b].rearrange("(m t) j -> m t j", t=T))
+            else:
+                nc.sync.dma_start(out=raw[x, b][:], in_=src[b].rearrange("(p t) c -> p t c", t=T))
+
+        nc.vector.memset(warm[:], 0.0)
+        with nc.allow_non_contiguous_dma(reason="512 single temperatures, one to a partition and query tile"):
+            nc.scalar.dma_start(out=temp_raw[:, :, 0:1], in_=temp.rearrange("(c p) -> p c", p=P).unsqueeze(2))
+        nc.scalar.activation(out=warm[:], in_=warm[:], func=ACT.Exp)
+        load("k", k, 0)
+        load("q", q, 0)
+        load("k", k, 1)
+        nc.sync.dma_start(out=u_raw[:], in_=u.partition_broadcast(P))
+        load("v", v, 0)
+        load("q", q, 1)
+        nc.sync.dma_start(out=zs_all[:].rearrange("p b c -> p (b c)"), in_=zs.rearrange("b c -> (b c)").partition_broadcast(P))
+        nc.sync.dma_start(out=zb_all[:].rearrange("p b c -> p (b c)"), in_=zb.rearrange("b c -> (b c)").partition_broadcast(P))
+        load("v", v, 1)
+
+        make_identity(nc, ident[:])
+        nc.gpsimd.memset(minus_half[:], -0.5)
+        nc.gpsimd.tensor_scalar(out=neg_temp[:], in0=temp_raw[:, :, 0:1], scalar1=-1.0 / math.sqrt(N), scalar2=0.0, op0=ALU.mult, op1=ALU.add)
+
+        def inter(eng, x, b, lo, hi):
+            dst = grouped[x, b][:, lo:hi, :]
+            src = raw[x, b][:, :, lo:hi].rearrange("p t c -> p c t")
+            if eng == "D":
+                nc.vector.tensor_copy(out=dst, in_=src)
+            elif eng == "G":
+                nc.gpsimd.tensor_scalar(out=dst, in0=src, scalar1=1.0, scalar2=0.0, op0=ALU.mult, op1=ALU.add)
+            else:
+                nc.scalar.copy(out=dst, in_=src)
+
+        def quant(x, b, lo, hi):
+            nc.vector.quantize_mx(
+                out=codes[x, b][:, lo:hi].bitcast(FP8X4), scales=scales[x, b][:, lo:hi],
+                in_=grouped[x, b][:, lo:hi, :].rearrange("p c t -> p (c t)"))
+
+        def mm(x, w, b, i):
+            acc = psum.tile([P, C], F32, name="acc")
+            cols = slice(i * P, (i + 1) * P)
+            nc.tensor.matmul_mx(
+                out=acc[:], lhsT=codes[x, b][:, cols].bitcast(FP8X4), lhsT_scale=scales[x, b][:, cols],
+                rhs=codes[w, b][:].bitcast(FP8X4), rhs_scale=scales[w, b][:], start=True, stop=True)
+            return acc
+
+        gram = {}
+        o = {}
+        bank = {}
+
+        def g(b, i):
+            gram[b, i] = mm("q", "k", b, i)
+
+        def rowmax(b, i):
+            nc.vector.tensor_scalar(
+                out=neg_a[b][i][:].rearrange("p (h m e) -> p h m e", h=2, e=2),
+                in0=gram[b, i][:].rearrange("p (m h e) -> p h m e", h=2, e=2),
+                scalar1=neg_temp[:, i, :], scalar2=None, op0=ALU.mult, op1=ALU.min, accum_out=neg_max[b][i][:])
+
+        def ex(b, i):
+            nc.scalar.activation(out=expo[b][i][:], in_=neg_a[b][i][:], func=ACT.Exp, bias=neg_max[b][i][:], scale=-1.0, accum_out=total[b][i // 2][:, i % 2:i % 2 + 1])
+
+        def rec(b, h):
+            nc.vector.reciprocal(out=inv_total[b][h][:], in_=total[b][h][:])
+
+        def mulu(b, i):
+            nc.vector.scalar_tensor_tensor(out=pu[b][i][:], in0=expo[b][i][:], scalar=inv_total[b][i // 2][:, i % 2:i % 2 + 1], in1=u_perm[:], op0=ALU.mult, op1=ALU.mult)
+
+        def new_bank(x, b, h):
+            bank[x, b, h] = turn.tile([P, 2, 2, P], F32, name="words")
+
+        def tp(b, i):
+            if i % 2 == 0:
+                new_bank("p", b, i // 2)
+            words = pu[b][i][:].bitcast(F32)
+            for h in range(2):
+                nc.tensor.transpose(bank["p", b, i // 2][:, i % 2, h, :], words[:, h * P:(h + 1) * P], ident[:])
+
+        def tv(b, t):
+            if t % 2 == 0:
+                new_bank("v", b, t // 2)
+            words = raw["v", b][:].rearrange("p t c -> p (t c)").bitcast(F32)
+            for h in range(2):
+                lo = t * (C // 2) + h
+                nc.tensor.transpose(bank["v", b, t // 2][:, t % 2, h, :], words[:, lo:(t + 1) * (C // 2):2], ident[:])
+
+        def cp(x, b, h):
+            dst = grouped[x, b][:, h * 2 * P:(h + 1) * 2 * P, :].rearrange("p c t -> p (c t)").bitcast(F32)
+            nc.scalar.copy(out=dst.rearrange("p (i m h) -> p i m h", i=2, h=2), in_=bank[x, b, h][:].rearrange("p i h m -> p i m h"))
+
+        def om(b, t):
+            o[b, t] = mm("v", "p", b, t)
+
+        def modz(b, t):
+            nc.vector.scalar_tensor_tensor(out=mod[b][:, t, :], in0=zs_all[:, b, :], scalar=1.0, in1=o[b, t][:], op0=ALU.add, op1=ALU.mult)
+
+        def sq(b, t):
+            nc.scalar.activation(out=junk[:], in_=o[b, t][:], func=ACT.Square, scale=1.0 / math.sqrt(C), accum_out=ms[b][t][:])
+
+        def rs(b, t):
+            nc.gpsimd.tensor_scalar(out=ms_eps[b][t][:], in0=ms[b][t][:], scalar1=EPS, scalar2=1.0, op0=ALU.add, op1=ALU.mult)
+            nc.gpsimd.tensor_tensor(out=rstd[b][t][:], in0=ms_eps[b][t][:], in1=minus_half[:], op=ALU.pow)
+
+        def fin(b, t, lo, hi):
+            nc.vector.scalar_tensor_tensor(
+                out=res[b][:, t, lo:hi], in0=mod[b][:, t, lo:hi], scalar=rstd[b][t][:], in1=zb_all[:, b, lo:hi], op0=ALU.mult, op1=ALU.add)
+
+        def st(b, t0, t1, lo, hi):
+            nc.sync.dma_start(out=out_0[b].rearrange("(p t) c -> p t c", t=T)[:, t0:t1, lo:hi], in_=res[b][:, t0:t1, lo:hi])
+
+        def ycopy(eng, b, lo, hi):
+            dst = grouped["y", b][:, lo:hi, :]
+            src = res[b][:, :, lo:hi].rearrange("p t c -> p c t")
+            if eng == "D":
+                nc.vector.tensor_copy(out=dst, in_=src)
+            else:
+                nc.scalar.copy(out=dst, in_=src)
+
+        def yquant(b, lo, hi):
+            nc.vector.quantize_mx(
+                out=y_codes[:, b, lo:hi].bitcast(FP8X4), scales=y_scales[:, b, lo:hi],
+                in_=grouped["y", b][:, lo:hi, :].rearrange("p c t -> p (c t)"))
+
+        words_out = out_1[0].rearrange("p m t -> p (m t)").bitcast(I32)
+        scales_out = out_2[0].bitcast(I32)
+
+        def st_words(b, lo, hi):
+            nc.sync.dma_start(out=words_out[:, b * C + lo:b * C + hi], in_=y_codes[:, b, lo:hi].bitcast(I32))
+
+        def st_scales(b, engines):
+            for Q in range(4):
+                engines[Q % len(engines)].dma_start(
+                    out=scales_out[4 * Q:4 * Q + 4, b * C // 4:(b + 1) * C // 4],
+                    in_=y_scales[32 * Q:32 * Q + 4, b, :].bitcast(I32))
+
+        def prep_u():
+            nc.gpsimd.tensor_scalar(
+                out=u_perm[:].rearrange("p (h m e) -> p h m e", h=2, e=2),
+                in0=u_raw[:].rearrange("p (m h e) -> p h m e", h=2, e=2),
+                scalar1=math.sqrt(C), scalar2=0.0, op0=ALU.mult, op1=ALU.add)
+
+
+        inter("D", "k", 0, 0, 352)
+        inter("A", "k", 0, 352, 512)
+        inter("D", "q", 0, 0, 256)
+        inter("A", "q", 0, 256, 512)
+        for c in range(T):
+            inter("G", "k", 1, c * P, (c + 1) * P)
+        prep_u()
+        quant("k", 0, 0, 512)
+        quant("q", 0, 0, 256)
+        quant("q", 0, 256, 512)
+        for i in range(T):
+            g(0, i)
+        for t in range(T):
+            tv(0, t)
+        rowmax(0, 0)
+        rowmax(0, 1)
+        ex(0, 0)
+        inter("D", "q", 1, 0, 256)
+        inter("A", "q", 1, 256, 512)
+        rowmax(0, 2)
+        ex(0, 1)
+        quant("k", 1, 0, 512)
+        rowmax(0, 3)
+        ex(0, 2)
+        quant("q", 1, 0, 256)
+        ex(0, 3)
+        quant("q", 1, 256, 512)
+        for i in range(T):
+            g(1, i)
+        cp("v", 0, 0)
+        rec(0, 0)
+        rowmax(1, 0)
+        mulu(0, 0)
+        tp(0, 0)
+        mulu(0, 1)
+        tp(0, 1)
+        cp("v", 0, 1)
+        rec(0, 1)
+        rowmax(1, 1)
+        ex(1, 0)
+        mulu(0, 2)
+        tp(0, 2)
+        cp("p", 0, 0)
+        mulu(0, 3)
+        tp(0, 3)
+        ex(1, 1)
+        rowmax(1, 2)
+        cp("p", 0, 1)
+        quant("v", 0, 0, 512)
+        rowmax(1, 3)
+        ex(1, 2)
+        quant("p", 0, 0, 256)
+        rec(1, 0)
+        ex(1, 3)
+        quant("p", 0, 256, 512)
+        for t in range(T):
+            tv(1, t)
+        for t in range(T):
+            om(0, t)
+        mulu(1, 0)
+        tp(1, 0)
+        mulu(1, 1)
+        tp(1, 1)
+        rec(1, 1)
+        cp("v", 1, 0)
+        cp("v", 1, 1)
+        modz(0, 0)
+        sq(0, 0)
+        mulu(1, 2)
+        tp(1, 2)
+        mulu(1, 3)
+        tp(1, 3)
+        cp("p", 1, 0)
+        quant("v", 1, 0, 512)
+        sq(0, 1)
+        modz(0, 1)
+        cp("p", 1, 1)
+        quant("p", 1, 0, 256)
+        sq(0, 2)
+        modz(0, 2)
+        sq(0, 3)
+        quant("p", 1, 256, 512)
+        modz(0, 3)
+        for t in range(T):
+            rs(0, t)
+        for t in range(T):
+            om(1, t)
+        for t in range(T):
+            fin(0, t, 0, 512)
+            modz(1, t)
+            sq(1, t)
+            rs(1, t)
+            if t % 2:
+                st(0, t - 1, t + 1, 0, 512)
+        ycopy("A", 0, 0, 256)
+        ycopy("A", 0, 256, 512)
+        for t in range(T):
+            fin(1, t, 0, 256)
+        ycopy("A", 1, 0, 128)
+        ycopy("A", 1, 128, 256)
+        for t in range(T):
+            fin(1, t, 256, 512)
+            if t % 2:
+                st(1, t - 1, t + 1, 0, 512)
+        yquant(0, 0, 512)
+        st_words(0, 0, 512)
+        st_scales(0, [nc.sync])
+        ycopy("A", 1, 256, 352)
+        ycopy("D", 1, 352, 512)
+        yquant(1, 0, 256)
+        st_words(1, 0, 256)
+        yquant(1, 256, 512)
+        st_scales(1, [nc.scalar])
+        st_words(1, 256, 512)

@@ -61,9 +61,9 @@ def tile_diffirpriorchannelattention_x1_kernel(tc, q, k, v, temp, u, zs, zb, out
         warm = sb([P, 1], F32, "warm")
         ident = sb([P, P], F32, "ident")
         minus_half = sb([P, 1], F32, "minus_half")
-        temp_raw = sb([P, T, 2], BF16, "temp_raw")
-        neg_temp = sb([P, T, 1], F32, "neg_temp")
-        u_raw = sb([P, C], BF16, "u_raw")
+        rows = sb([P, C], BF16, "rows")
+        ident_b = sb([P, P], BF16, "ident_b")
+        neg_temp = sb([P, T], F32, "neg_temp")
         u_perm = sb([P, C], F32, "u_perm")
         zs_all = sb([P, B, C], BF16, "zs_all")
         zb_all = sb([P, B, C], BF16, "zb_all")
@@ -74,31 +74,29 @@ def tile_diffirpriorchannelattention_x1_kernel(tc, q, k, v, temp, u, zs, zb, out
             else:
                 nc.sync.dma_start(out=raw[x, b][:], in_=src[b].rearrange("(p t) c -> p t c", t=T))
 
+        nc.gpsimd.memset(rows[:].bitcast(I32), 0)
         nc.vector.memset(warm[:], 0.0)
-        with nc.allow_non_contiguous_dma(reason="512 single temperatures, one to a partition and query tile"):
-            nc.scalar.dma_start(out=temp_raw[:, :, 0:1], in_=temp.rearrange("(c p) -> p c", p=P).unsqueeze(2))
-        nc.scalar.activation(out=warm[:], in_=warm[:], func=ACT.Exp)
         load("k", k, 0)
+        nc.sync.dma_start(out=rows[0:1, :], in_=u.unsqueeze(0))
+        nc.sync.dma_start(out=rows[1:1 + T, 0:P], in_=temp.rearrange("(c p) -> c p", p=P))
         load("q", q, 0)
+        nc.scalar.activation(out=warm[:], in_=warm[:], func=ACT.Exp)
         load("k", k, 1)
-        nc.sync.dma_start(out=u_raw[:], in_=u.partition_broadcast(P))
         load("v", v, 0)
         load("q", q, 1)
+        load("v", v, 1)
         nc.sync.dma_start(out=zs_all[:].rearrange("p b c -> p (b c)"), in_=zs.rearrange("b c -> (b c)").partition_broadcast(P))
         nc.sync.dma_start(out=zb_all[:].rearrange("p b c -> p (b c)"), in_=zb.rearrange("b c -> (b c)").partition_broadcast(P))
-        load("v", v, 1)
 
+        make_identity(nc, ident_b[:])
         make_identity(nc, ident[:])
         nc.gpsimd.memset(minus_half[:], -0.5)
-        nc.gpsimd.tensor_scalar(out=neg_temp[:], in0=temp_raw[:, :, 0:1], scalar1=-1.0 / math.sqrt(N), scalar2=0.0, op0=ALU.mult, op1=ALU.add)
 
         def inter(eng, x, b, lo, hi):
             dst = grouped[x, b][:, lo:hi, :]
             src = raw[x, b][:, :, lo:hi].rearrange("p t c -> p c t")
             if eng == "D":
                 nc.vector.tensor_copy(out=dst, in_=src)
-            elif eng == "G":
-                nc.gpsimd.tensor_scalar(out=dst, in0=src, scalar1=1.0, scalar2=0.0, op0=ALU.mult, op1=ALU.add)
             else:
                 nc.scalar.copy(out=dst, in_=src)
 
@@ -126,7 +124,7 @@ def tile_diffirpriorchannelattention_x1_kernel(tc, q, k, v, temp, u, zs, zb, out
             nc.vector.tensor_scalar(
                 out=neg_a[b][i][:].rearrange("p (h m e) -> p h m e", h=2, e=2),
                 in0=gram[b, i][:].rearrange("p (m h e) -> p h m e", h=2, e=2),
-                scalar1=neg_temp[:, i, :], scalar2=None, op0=ALU.mult, op1=ALU.min, accum_out=neg_max[b][i][:])
+                scalar1=neg_temp[:, i:i + 1], scalar2=None, op0=ALU.mult, op1=ALU.min, accum_out=neg_max[b][i][:])
 
         def ex(b, i):
             nc.scalar.activation(out=expo[b][i][:], in_=neg_a[b][i][:], func=ACT.Exp, bias=neg_max[b][i][:], scale=-1.0, accum_out=total[b][i // 2][:, i % 2:i % 2 + 1])
@@ -204,40 +202,51 @@ def tile_diffirpriorchannelattention_x1_kernel(tc, q, k, v, temp, u, zs, zb, out
                     out=scales_out[4 * Q:4 * Q + 4, b * C // 4:(b + 1) * C // 4],
                     in_=y_scales[32 * Q:32 * Q + 4, b, :].bitcast(I32))
 
+        small = {}
+
+        def spread():
+            small["u"] = psum.tile([P, C], F32, name="acc")
+            nc.tensor.matmul(small["u"][:], lhsT=ident_b[:, 0:1].to_broadcast([P, P]), rhs=rows[:], start=True, stop=True)
+            small["t"] = turn.tile([P, P], BF16, name="words")
+            nc.tensor.transpose(small["t"][:], rows[:, 0:P], ident_b[:])
+
+        def prep_temp():
+            nc.vector.tensor_scalar(out=neg_temp[:], in0=small["t"][:, 1:1 + T], scalar1=-1.0 / math.sqrt(N), scalar2=None, op0=ALU.mult)
+
         def prep_u():
-            nc.gpsimd.tensor_scalar(
+            nc.scalar.activation(
                 out=u_perm[:].rearrange("p (h m e) -> p h m e", h=2, e=2),
-                in0=u_raw[:].rearrange("p (m h e) -> p h m e", h=2, e=2),
-                scalar1=math.sqrt(C), scalar2=0.0, op0=ALU.mult, op1=ALU.add)
+                in_=small["u"][:].rearrange("p (m h e) -> p h m e", h=2, e=2), func=ACT.Copy, scale=math.sqrt(C))
 
-
+        spread()
         inter("D", "k", 0, 0, 352)
         inter("A", "k", 0, 352, 512)
         inter("D", "q", 0, 0, 256)
         inter("A", "q", 0, 256, 512)
-        for c in range(T):
-            inter("G", "k", 1, c * P, (c + 1) * P)
         prep_u()
         quant("k", 0, 0, 512)
+        prep_temp()
         quant("q", 0, 0, 256)
         quant("q", 0, 256, 512)
         for i in range(T):
             g(0, i)
         for t in range(T):
             tv(0, t)
+        inter("D", "k", 1, 0, 256)
+        inter("A", "k", 1, 256, 512)
         rowmax(0, 0)
-        rowmax(0, 1)
+        quant("k", 1, 0, 512)
         ex(0, 0)
-        inter("D", "q", 1, 0, 256)
+        rowmax(0, 1)
         inter("A", "q", 1, 256, 512)
         rowmax(0, 2)
         ex(0, 1)
-        quant("k", 1, 0, 512)
-        rowmax(0, 3)
+        inter("D", "q", 1, 0, 256)
         ex(0, 2)
-        quant("q", 1, 0, 256)
-        ex(0, 3)
+        rowmax(0, 3)
         quant("q", 1, 256, 512)
+        ex(0, 3)
+        quant("q", 1, 0, 256)
         for i in range(T):
             g(1, i)
         cp("v", 0, 0)
@@ -309,19 +318,21 @@ def tile_diffirpriorchannelattention_x1_kernel(tc, q, k, v, temp, u, zs, zb, out
         ycopy("A", 0, 256, 512)
         for t in range(T):
             fin(1, t, 0, 256)
+        st(1, 0, T, 0, 256)
         ycopy("A", 1, 0, 128)
         ycopy("A", 1, 128, 256)
         for t in range(T):
             fin(1, t, 256, 512)
+            if t == 1:
+                yquant(0, 0, 512)
+                st_words(0, 0, 512)
+                st_scales(0, [nc.sync])
             if t % 2:
-                st(1, t - 1, t + 1, 0, 512)
-        yquant(0, 0, 512)
-        st_words(0, 0, 512)
-        st_scales(0, [nc.sync])
+                st(1, t - 1, t + 1, 256, 512)
         ycopy("A", 1, 256, 352)
         ycopy("D", 1, 352, 512)
         yquant(1, 0, 256)
         st_words(1, 0, 256)
         yquant(1, 256, 512)
-        st_scales(1, [nc.scalar])
         st_words(1, 256, 512)
+        st_scales(1, [nc.scalar, nc.sync])

@@ -54,13 +54,13 @@ def tile_diffirpriorchannelattention_x1_kernel(tc, q, k, v, temp, u, zs, zb, out
         neg_max = [[sb([P, 1], F32, f"neg_max{b}_{i}") for i in range(T)] for b in range(B)]
         total = [[sb([P, 2], F32, f"total{b}_{h}") for h in range(2)] for b in range(B)]
         inv_total = [[sb([P, 2], F32, f"inv_total{b}_{h}") for h in range(2)] for b in range(B)]
-        ms = [[sb([P, 1], F32, f"ms{b}_{t}") for t in range(T)] for b in range(B)]
-        ms_eps = [[sb([P, 1], F32, f"ms_eps{b}_{t}") for t in range(T)] for b in range(B)]
-        rstd = [[sb([P, 1], F32, f"rstd{b}_{t}") for t in range(T)] for b in range(B)]
+        ms = [[sb([P, 2], F32, f"ms{b}_{h}") for h in range(2)] for b in range(B)]
+        rstd = [[sb([P, 2], F32, f"rstd{b}_{h}") for h in range(2)] for b in range(B)]
         junk = sb([P, C], F32, "junk")
         warm = sb([P, 1], F32, "warm")
         ident = sb([P, P], F32, "ident")
-        minus_half = sb([P, 1], F32, "minus_half")
+        zero = sb([P, 1], F32, "zero")
+        eps = sb([P, 1], F32, "eps")
         rows = sb([P, C], BF16, "rows")
         ident_b = sb([P, P], BF16, "ident_b")
         neg_temp = sb([P, T], F32, "neg_temp")
@@ -90,7 +90,8 @@ def tile_diffirpriorchannelattention_x1_kernel(tc, q, k, v, temp, u, zs, zb, out
 
         make_identity(nc, ident_b[:])
         make_identity(nc, ident[:])
-        nc.gpsimd.memset(minus_half[:], -0.5)
+        nc.gpsimd.memset(zero[:], 0.0)
+        nc.gpsimd.tensor_scalar(out=eps[:], in0=zero[:], scalar1=EPS, scalar2=1.0, op0=ALU.add, op1=ALU.mult)
 
         def inter(eng, x, b, lo, hi):
             dst = grouped[x, b][:, lo:hi, :]
@@ -164,15 +165,14 @@ def tile_diffirpriorchannelattention_x1_kernel(tc, q, k, v, temp, u, zs, zb, out
             nc.vector.scalar_tensor_tensor(out=mod[b][:, t, :], in0=zs_all[:, b, :], scalar=1.0, in1=o[b, t][:], op0=ALU.add, op1=ALU.mult)
 
         def sq(b, t):
-            nc.scalar.activation(out=junk[:], in_=o[b, t][:], func=ACT.Square, scale=1.0 / math.sqrt(C), accum_out=ms[b][t][:])
+            nc.scalar.activation(out=junk[:], in_=o[b, t][:], func=ACT.Square, scale=1.0 / math.sqrt(C), accum_out=ms[b][t // 2][:, t % 2:t % 2 + 1])
 
-        def rs(b, t):
-            nc.gpsimd.tensor_scalar(out=ms_eps[b][t][:], in0=ms[b][t][:], scalar1=EPS, scalar2=1.0, op0=ALU.add, op1=ALU.mult)
-            nc.gpsimd.tensor_tensor(out=rstd[b][t][:], in0=ms_eps[b][t][:], in1=minus_half[:], op=ALU.pow)
+        def rs(b, h):
+            nc.scalar.activation(out=rstd[b][h][:], in_=ms[b][h][:], func=ACT.Abs_reciprocal_sqrt, bias=eps[:])
 
         def fin(b, t, lo, hi):
             nc.vector.scalar_tensor_tensor(
-                out=res[b][:, t, lo:hi], in0=mod[b][:, t, lo:hi], scalar=rstd[b][t][:], in1=zb_all[:, b, lo:hi], op0=ALU.mult, op1=ALU.add)
+                out=res[b][:, t, lo:hi], in0=mod[b][:, t, lo:hi], scalar=rstd[b][t // 2][:, t % 2:t % 2 + 1], in1=zb_all[:, b, lo:hi], op0=ALU.mult, op1=ALU.add)
 
         def st(b, t0, t1, lo, hi):
             nc.sync.dma_start(out=out_0[b].rearrange("(p t) c -> p t c", t=T)[:, t0:t1, lo:hi], in_=res[b][:, t0:t1, lo:hi])
@@ -196,11 +196,14 @@ def tile_diffirpriorchannelattention_x1_kernel(tc, q, k, v, temp, u, zs, zb, out
         def st_words(b, lo, hi):
             nc.sync.dma_start(out=words_out[:, b * C + lo:b * C + hi], in_=y_codes[:, b, lo:hi].bitcast(I32))
 
-        def st_scales(b, engines):
+        def st_scales(engines):
             for Q in range(4):
                 engines[Q % len(engines)].dma_start(
-                    out=scales_out[4 * Q:4 * Q + 4, b * C // 4:(b + 1) * C // 4],
-                    in_=y_scales[32 * Q:32 * Q + 4, b, :].bitcast(I32))
+                    out=scales_out[4 * Q:4 * Q + 4, :],
+                    in_=y_scales[32 * Q:32 * Q + 4, :, :].rearrange("p b c -> p (b c)").bitcast(I32))
+
+        def warm_root():
+            nc.scalar.activation(out=warm[:], in_=zero[:], func=ACT.Abs_reciprocal_sqrt, bias=eps[:])
 
         small = {}
 
@@ -251,9 +254,9 @@ def tile_diffirpriorchannelattention_x1_kernel(tc, q, k, v, temp, u, zs, zb, out
             g(1, i)
         cp("v", 0, 0)
         rec(0, 0)
-        rowmax(1, 0)
         mulu(0, 0)
         tp(0, 0)
+        rowmax(1, 0)
         mulu(0, 1)
         tp(0, 1)
         cp("v", 0, 1)
@@ -286,6 +289,7 @@ def tile_diffirpriorchannelattention_x1_kernel(tc, q, k, v, temp, u, zs, zb, out
         rec(1, 1)
         cp("v", 1, 0)
         cp("v", 1, 1)
+        warm_root()
         modz(0, 0)
         sq(0, 0)
         mulu(1, 2)
@@ -298,22 +302,24 @@ def tile_diffirpriorchannelattention_x1_kernel(tc, q, k, v, temp, u, zs, zb, out
         modz(0, 1)
         cp("p", 1, 1)
         quant("p", 1, 0, 256)
+        rs(0, 0)
         sq(0, 2)
         modz(0, 2)
         sq(0, 3)
+        rs(0, 1)
         quant("p", 1, 256, 512)
         modz(0, 3)
-        for t in range(T):
-            rs(0, t)
         for t in range(T):
             om(1, t)
         for t in range(T):
             fin(0, t, 0, 512)
-            modz(1, t)
-            sq(1, t)
-            rs(1, t)
             if t % 2:
                 st(0, t - 1, t + 1, 0, 512)
+        for t in range(T):
+            modz(1, t)
+            sq(1, t)
+            if t % 2:
+                rs(1, t // 2)
         ycopy("A", 0, 0, 256)
         ycopy("A", 0, 256, 512)
         for t in range(T):
@@ -326,7 +332,6 @@ def tile_diffirpriorchannelattention_x1_kernel(tc, q, k, v, temp, u, zs, zb, out
             if t == 1:
                 yquant(0, 0, 512)
                 st_words(0, 0, 512)
-                st_scales(0, [nc.sync])
             if t % 2:
                 st(1, t - 1, t + 1, 256, 512)
         ycopy("A", 1, 256, 352)
@@ -335,4 +340,4 @@ def tile_diffirpriorchannelattention_x1_kernel(tc, q, k, v, temp, u, zs, zb, out
         st_words(1, 0, 256)
         yquant(1, 256, 512)
         st_words(1, 256, 512)
-        st_scales(1, [nc.scalar, nc.sync])
+        st_scales([nc.scalar, nc.sync])

@@ -77,9 +77,9 @@ def tile_diffirpriorchannelattention_x1_kernel(tc, q, k, v, temp, u, zs, zb, out
         nc.gpsimd.memset(rows[:].bitcast(I32), 0)
         nc.vector.memset(warm[:], 0.0)
         load("k", k, 0)
+        load("q", q, 0)
         nc.sync.dma_start(out=rows[0:1, :], in_=u.unsqueeze(0))
         nc.sync.dma_start(out=rows[1:1 + T, 0:P], in_=temp.rearrange("(c p) -> c p", p=P))
-        load("q", q, 0)
         nc.scalar.activation(out=warm[:], in_=warm[:], func=ACT.Exp)
         load("k", k, 1)
         load("v", v, 0)
@@ -94,8 +94,8 @@ def tile_diffirpriorchannelattention_x1_kernel(tc, q, k, v, temp, u, zs, zb, out
         nc.gpsimd.tensor_scalar(out=eps[:], in0=zero[:], scalar1=EPS, scalar2=1.0, op0=ALU.add, op1=ALU.mult)
 
         def inter(eng, x, b, lo, hi):
-            dst = grouped[x, b][:, lo:hi, :]
-            src = raw[x, b][:, :, lo:hi].rearrange("p t c -> p c t")
+            dst = grouped[x, b][:, lo:hi, :].rearrange("p (c i) t -> p c t i", i=4)
+            src = raw[x, b][:, :, lo:hi].rearrange("p t (c i) -> p c t i", i=4)
             if eng == "D":
                 nc.vector.tensor_copy(out=dst, in_=src)
             else:
@@ -178,8 +178,8 @@ def tile_diffirpriorchannelattention_x1_kernel(tc, q, k, v, temp, u, zs, zb, out
             nc.sync.dma_start(out=out_0[b].rearrange("(p t) c -> p t c", t=T)[:, t0:t1, lo:hi], in_=res[b][:, t0:t1, lo:hi])
 
         def ycopy(eng, b, lo, hi):
-            dst = grouped["y", b][:, lo:hi, :]
-            src = res[b][:, :, lo:hi].rearrange("p t c -> p c t")
+            dst = grouped["y", b][:, lo:hi, :].rearrange("p (c i) t -> p c t i", i=4)
+            src = res[b][:, :, lo:hi].rearrange("p t (c i) -> p c t i", i=4)
             if eng == "D":
                 nc.vector.tensor_copy(out=dst, in_=src)
             else:
@@ -228,7 +228,6 @@ def tile_diffirpriorchannelattention_x1_kernel(tc, q, k, v, temp, u, zs, zb, out
         inter("A", "q", 0, 256, 512)
         prep_u()
         quant("k", 0, 0, 512)
-        prep_temp()
         quant("q", 0, 0, 256)
         quant("q", 0, 256, 512)
         for i in range(T):
@@ -237,6 +236,7 @@ def tile_diffirpriorchannelattention_x1_kernel(tc, q, k, v, temp, u, zs, zb, out
             tv(0, t)
         inter("D", "k", 1, 0, 256)
         inter("A", "k", 1, 256, 512)
+        prep_temp()
         rowmax(0, 0)
         quant("k", 1, 0, 512)
         ex(0, 0)

@@ -25,8 +25,8 @@ def tile_diffirpriorchannelattention_x1_kernel(tc, q, k, v, temp, u, zs, zb, out
     nc = tc.nc
     with ExitStack() as ctx:
         keep = ctx.enter_context(tc.tile_pool(name="keep", bufs=1))
-        psum = ctx.enter_context(tc.psum_pool(name="psum", bufs=6))
-        turn = ctx.enter_context(tc.psum_pool(name="turn", bufs=2))
+        psum = ctx.enter_context(tc.psum_pool(name="psum", bufs=5))
+        turn = ctx.enter_context(tc.psum_pool(name="turn", bufs=3))
         ctx.enter_context(tc.manual_schedule())
 
         def sb(shape, dtype, name):
@@ -82,8 +82,8 @@ def tile_diffirpriorchannelattention_x1_kernel(tc, q, k, v, temp, u, zs, zb, out
         nc.sync.dma_start(out=rows[1:1 + T, 0:P], in_=temp.rearrange("(c p) -> c p", p=P))
         nc.scalar.activation(out=warm[:], in_=warm[:], func=ACT.Exp)
         load("k", k, 1)
-        load("v", v, 0)
         load("q", q, 1)
+        load("v", v, 0)
         load("v", v, 1)
         nc.sync.dma_start(out=zs_all[:].rearrange("p b c -> p (b c)"), in_=zs.rearrange("b c -> (b c)").partition_broadcast(P))
         nc.sync.dma_start(out=zb_all[:].rearrange("p b c -> p (b c)"), in_=zb.rearrange("b c -> (b c)").partition_broadcast(P))
@@ -207,9 +207,11 @@ def tile_diffirpriorchannelattention_x1_kernel(tc, q, k, v, temp, u, zs, zb, out
 
         small = {}
 
-        def spread():
+        def spread_u():
             small["u"] = psum.tile([P, C], F32, name="acc")
             nc.tensor.matmul(small["u"][:], lhsT=ident_b[:, 0:1].to_broadcast([P, P]), rhs=rows[:], start=True, stop=True)
+
+        def spread_temp():
             small["t"] = turn.tile([P, P], BF16, name="words")
             nc.tensor.transpose(small["t"][:], rows[:, 0:P], ident_b[:])
 
@@ -221,102 +223,107 @@ def tile_diffirpriorchannelattention_x1_kernel(tc, q, k, v, temp, u, zs, zb, out
                 out=u_perm[:].rearrange("p (h m e) -> p h m e", h=2, e=2),
                 in_=small["u"][:].rearrange("p (m h e) -> p h m e", h=2, e=2), func=ACT.Copy, scale=math.sqrt(C))
 
-        spread()
+        spread_temp()
         inter("D", "k", 0, 0, 352)
         inter("A", "k", 0, 352, 512)
         inter("D", "q", 0, 0, 256)
         inter("A", "q", 0, 256, 512)
-        prep_u()
         quant("k", 0, 0, 512)
         quant("q", 0, 0, 256)
-        quant("q", 0, 256, 512)
-        for i in range(T):
-            g(0, i)
-        for t in range(T):
-            tv(0, t)
         inter("D", "k", 1, 0, 256)
         inter("A", "k", 1, 256, 512)
         prep_temp()
+        quant("q", 0, 256, 512)
+        for i in range(T):
+            g(0, i)
+        spread_u()
+        inter("A", "q", 1, 0, 256)
         rowmax(0, 0)
         quant("k", 1, 0, 512)
-        ex(0, 0)
         rowmax(0, 1)
         inter("A", "q", 1, 256, 512)
+        ex(0, 0)
         rowmax(0, 2)
+        quant("q", 1, 0, 256)
         ex(0, 1)
-        inter("D", "q", 1, 0, 256)
-        ex(0, 2)
+        prep_u()
         rowmax(0, 3)
         quant("q", 1, 256, 512)
-        ex(0, 3)
-        quant("q", 1, 0, 256)
         for i in range(T):
             g(1, i)
+        for t in range(T):
+            tv(0, t)
+        ex(0, 2)
+        ex(0, 3)
         cp("v", 0, 0)
+        rowmax(1, 0)
+        rowmax(1, 1)
         rec(0, 0)
+        rowmax(1, 2)
+        ex(1, 0)
+        cp("v", 0, 1)
         mulu(0, 0)
         tp(0, 0)
-        rowmax(1, 0)
         mulu(0, 1)
         tp(0, 1)
-        cp("v", 0, 1)
         rec(0, 1)
-        rowmax(1, 1)
-        ex(1, 0)
+        ex(1, 1)
+        rowmax(1, 3)
+        cp("p", 0, 0)
         mulu(0, 2)
         tp(0, 2)
-        cp("p", 0, 0)
         mulu(0, 3)
         tp(0, 3)
-        ex(1, 1)
-        rowmax(1, 2)
+        ex(1, 2)
+        ex(1, 3)
         cp("p", 0, 1)
         quant("v", 0, 0, 512)
-        rowmax(1, 3)
-        ex(1, 2)
-        quant("p", 0, 0, 256)
         rec(1, 0)
-        ex(1, 3)
-        quant("p", 0, 256, 512)
+        quant("p", 0, 0, 256)
         for t in range(T):
             tv(1, t)
-        for t in range(T):
-            om(0, t)
         mulu(1, 0)
         tp(1, 0)
+        rec(1, 1)
         mulu(1, 1)
         tp(1, 1)
-        rec(1, 1)
+        quant("p", 0, 256, 512)
         cp("v", 1, 0)
         cp("v", 1, 1)
         warm_root()
-        modz(0, 0)
-        sq(0, 0)
+        for t in range(T):
+            om(0, t)
         mulu(1, 2)
         tp(1, 2)
         mulu(1, 3)
         tp(1, 3)
-        cp("p", 1, 0)
         quant("v", 1, 0, 512)
-        sq(0, 1)
+        cp("p", 1, 0)
+        sq(0, 0)
+        modz(0, 0)
         modz(0, 1)
         cp("p", 1, 1)
         quant("p", 1, 0, 256)
-        rs(0, 0)
-        sq(0, 2)
         modz(0, 2)
-        sq(0, 3)
-        rs(0, 1)
         quant("p", 1, 256, 512)
         modz(0, 3)
+        sq(0, 1)
+        rs(0, 0)
+        sq(0, 2)
+        sq(0, 3)
+        rs(0, 1)
         for t in range(T):
             om(1, t)
+        fin(0, 0, 0, 512)
+        fin(0, 1, 0, 512)
+        st(0, 0, 2, 0, 512)
+        modz(1, 0)
+        fin(0, 2, 0, 512)
+        fin(0, 3, 0, 512)
+        st(0, 2, 4, 0, 512)
         for t in range(T):
-            fin(0, t, 0, 512)
-            if t % 2:
-                st(0, t - 1, t + 1, 0, 512)
-        for t in range(T):
-            modz(1, t)
+            if t > 0:
+                modz(1, t)
             sq(1, t)
             if t % 2:
                 rs(1, t // 2)
@@ -335,9 +342,9 @@ def tile_diffirpriorchannelattention_x1_kernel(tc, q, k, v, temp, u, zs, zb, out
             if t % 2:
                 st(1, t - 1, t + 1, 256, 512)
         ycopy("A", 1, 256, 352)
-        ycopy("D", 1, 352, 512)
         yquant(1, 0, 256)
         st_words(1, 0, 256)
+        ycopy("D", 1, 352, 512)
         yquant(1, 256, 512)
         st_words(1, 256, 512)
         st_scales([nc.scalar, nc.sync])

import math
from contextlib import ExitStack

import concourse.mybir as mybir
from concourse.masks import make_identity

B, N, C = 2, 512, 512
EPS = 1e-6
FLOPS = B * 2 * (2 * N * C * C)

F32 = mybir.dt.float32
BF16 = mybir.dt.bfloat16
I32 = mybir.dt.int32
U32 = mybir.dt.uint32
U8 = mybir.dt.uint8
FP8X4 = mybir.dt.float8_e4m3fn_x4
ALU = mybir.AluOpType
ACT = mybir.ActivationFunctionType

P = 128
T = 4


def tile_diffirpriorchannelattention_x1_kernel(tc, q, k, v, temp, u, zs, zb, out_0, out_1, out_2):
    nc = tc.nc
    with ExitStack() as ctx:
        keep = ctx.enter_context(tc.tile_pool(name="keep", bufs=1))
        psum = ctx.enter_context(tc.psum_pool(name="psum", bufs=5))
        turn = ctx.enter_context(tc.psum_pool(name="turn", bufs=3))
        ctx.enter_context(tc.manual_schedule())

        def sb(shape, dtype, name):
            return keep.tile(shape, dtype, name=name, align_bytes=64)

        raw = {}
        grouped = {}
        codes = {}
        scales = {}
        for b in range(B):
            for x in "qkv":
                raw[x, b] = sb([P, T, C], BF16, f"raw_{x}{b}")
            for x in "qkvp":
                grouped[x, b] = sb([P, C, T], BF16, f"grouped_{x}{b}")
                codes[x, b] = sb([P, C], U32, f"codes_{x}{b}")
                scales[x, b] = sb([P, C], U8, f"scales_{x}{b}")
            grouped["y", b] = sb([P, C, T], BF16, f"grouped_y{b}")
        y_codes = sb([P, B, C], U32, "y_codes")
        y_scales = sb([P, B, C], U8, "y_scales")
        neg_a = [[sb([P, C], F32, f"neg_a{b}_{i}") for i in range(T)] for b in range(B)]
        expo = [[sb([P, C], F32, f"expo{b}_{i}") for i in range(T)] for b in range(B)]
        pu = [[sb([P, C], BF16, f"pu{b}_{i}") for i in range(T)] for b in range(B)]
        mod = [sb([P, T, C], F32, f"mod{b}") for b in range(B)]
        res = [sb([P, T, C], F32, f"res{b}") for b in range(B)]
        neg_max = [[sb([P, 1], F32, f"neg_max{b}_{i}") for i in range(T)] for b in range(B)]
        total = [[sb([P, 2], F32, f"total{b}_{h}") for h in range(2)] for b in range(B)]
        inv_total = [[sb([P, 2], F32, f"inv_total{b}_{h}") for h in range(2)] for b in range(B)]
        ms = [[sb([P, 2], F32, f"ms{b}_{h}") for h in range(2)] for b in range(B)]
        rstd = [[sb([P, 2], F32, f"rstd{b}_{h}") for h in range(2)] for b in range(B)]
        junk = sb([P, C], F32, "junk")
        warm = sb([P, 1], F32, "warm")
        ident = sb([P, P], F32, "ident")
        zero = sb([P, 1], F32, "zero")
        eps = sb([P, 1], F32, "eps")
        rows = sb([P, C], BF16, "rows")
        ident_b = sb([P, P], BF16, "ident_b")
        neg_temp = sb([P, T], F32, "neg_temp")
        u_perm = sb([P, C], F32, "u_perm")
        zs_all = sb([P, B, C], BF16, "zs_all")
        zb_all = sb([P, B, C], BF16, "zb_all")

        def load(x, src, b):
            if x == "v":
                nc.sync.dma_start(out=raw[x, b][:], in_=src[b].rearrange("(m t) j -> m t j", t=T))
            else:
                nc.sync.dma_start(out=raw[x, b][:], in_=src[b].rearrange("(p t) c -> p t c", t=T))

        nc.gpsimd.memset(rows[:].bitcast(I32), 0)
        nc.vector.memset(warm[:], 0.0)
        load("k", k, 0)
        load("q", q, 0)
        nc.sync.dma_start(out=rows[0:1, :], in_=u.unsqueeze(0))
        nc.sync.dma_start(out=rows[1:1 + T, 0:P], in_=temp.rearrange("(c p) -> c p", p=P))
        nc.scalar.activation(out=warm[:], in_=warm[:], func=ACT.Exp)
        load("k", k, 1)
        load("q", q, 1)
        load("v", v, 0)
        load("v", v, 1)
        nc.sync.dma_start(out=zs_all[:].rearrange("p b c -> p (b c)"), in_=zs.rearrange("b c -> (b c)").partition_broadcast(P))
        nc.sync.dma_start(out=zb_all[:].rearrange("p b c -> p (b c)"), in_=zb.rearrange("b c -> (b c)").partition_broadcast(P))

        make_identity(nc, ident_b[:])
        make_identity(nc, ident[:])
        nc.gpsimd.memset(zero[:], 0.0)
        nc.gpsimd.tensor_scalar(out=eps[:], in0=zero[:], scalar1=EPS, scalar2=1.0, op0=ALU.add, op1=ALU.mult)

        def inter(eng, x, b, lo, hi):
            dst = grouped[x, b][:, lo:hi, :].rearrange("p (c i) t -> p c t i", i=4)
            src = raw[x, b][:, :, lo:hi].rearrange("p t (c i) -> p c t i", i=4)
            if eng == "D":
                nc.vector.tensor_copy(out=dst, in_=src)
            else:
                nc.scalar.copy(out=dst, in_=src)

        def quant(x, b, lo, hi):
            nc.vector.quantize_mx(
                out=codes[x, b][:, lo:hi].bitcast(FP8X4), scales=scales[x, b][:, lo:hi],
                in_=grouped[x, b][:, lo:hi, :].rearrange("p c t -> p (c t)"))

        def mm(x, w, b, i):
            acc = psum.tile([P, C], F32, name="acc")
            cols = slice(i * P, (i + 1) * P)
            nc.tensor.matmul_mx(
                out=acc[:], lhsT=codes[x, b][:, cols].bitcast(FP8X4), lhsT_scale=scales[x, b][:, cols],
                rhs=codes[w, b][:].bitcast(FP8X4), rhs_scale=scales[w, b][:], start=True, stop=True)
            return acc

        gram = {}
        o = {}
        bank = {}

        def g(b, i):
            gram[b, i] = mm("q", "k", b, i)

        def rowmax(b, i):
            nc.vector.tensor_scalar(
                out=neg_a[b][i][:].rearrange("p (h m e) -> p h m e", h=2, e=2),
                in0=gram[b, i][:].rearrange("p (m h e) -> p h m e", h=2, e=2),
                scalar1=neg_temp[:, i:i + 1], scalar2=None, op0=ALU.mult, op1=ALU.min, accum_out=neg_max[b][i][:])

        def ex(b, i):
            nc.scalar.activation(out=expo[b][i][:], in_=neg_a[b][i][:], func=ACT.Exp, bias=neg_max[b][i][:], scale=-1.0, accum_out=total[b][i // 2][:, i % 2:i % 2 + 1])

        def rec(b, h):
            nc.vector.reciprocal(out=inv_total[b][h][:], in_=total[b][h][:])

        def mulu(b, i):
            nc.vector.scalar_tensor_tensor(out=pu[b][i][:], in0=expo[b][i][:], scalar=inv_total[b][i // 2][:, i % 2:i % 2 + 1], in1=u_perm[:], op0=ALU.mult, op1=ALU.mult)

        def new_bank(x, b, h):
            bank[x, b, h] = turn.tile([P, 2, 2, P], F32, name="words")

        def tp(b, i):
            if i % 2 == 0:
                new_bank("p", b, i // 2)
            words = pu[b][i][:].bitcast(F32)
            for h in range(2):
                nc.tensor.transpose(bank["p", b, i // 2][:, i % 2, h, :], words[:, h * P:(h + 1) * P], ident[:])

        def tv(b, t):
            if t % 2 == 0:
                new_bank("v", b, t // 2)
            words = raw["v", b][:].rearrange("p t c -> p (t c)").bitcast(F32)
            for h in range(2):
                lo = t * (C // 2) + h
                nc.tensor.transpose(bank["v", b, t // 2][:, t % 2, h, :], words[:, lo:(t + 1) * (C // 2):2], ident[:])

        def cp(x, b, h):
            dst = grouped[x, b][:, h * 2 * P:(h + 1) * 2 * P, :].rearrange("p c t -> p (c t)").bitcast(F32)
            nc.scalar.copy(out=dst.rearrange("p (i m h) -> p i m h", i=2, h=2), in_=bank[x, b, h][:].rearrange("p i h m -> p i m h"))

        def om(b, t):
            o[b, t] = mm("v", "p", b, t)

        def modz(b, t):
            nc.vector.scalar_tensor_tensor(out=mod[b][:, t, :], in0=zs_all[:, b, :], scalar=1.0, in1=o[b, t][:], op0=ALU.add, op1=ALU.mult)

        def sq(b, t):
            nc.scalar.activation(out=junk[:], in_=o[b, t][:], func=ACT.Square, scale=1.0 / math.sqrt(C), accum_out=ms[b][t // 2][:, t % 2:t % 2 + 1])

        def rs(b, h):
            nc.scalar.activation(out=rstd[b][h][:], in_=ms[b][h][:], func=ACT.Abs_reciprocal_sqrt, bias=eps[:])

        def fin(b, t, lo, hi):
            nc.vector.scalar_tensor_tensor(
                out=res[b][:, t, lo:hi], in0=mod[b][:, t, lo:hi], scalar=rstd[b][t // 2][:, t % 2:t % 2 + 1], in1=zb_all[:, b, lo:hi], op0=ALU.mult, op1=ALU.add)

        def st(b, t0, t1, lo, hi):
            nc.sync.dma_start(out=out_0[b].rearrange("(p t) c -> p t c", t=T)[:, t0:t1, lo:hi], in_=res[b][:, t0:t1, lo:hi])

        def ycopy(eng, b, lo, hi):
            dst = grouped["y", b][:, lo:hi, :].rearrange("p (c i) t -> p c t i", i=4)
            src = res[b][:, :, lo:hi].rearrange("p t (c i) -> p c t i", i=4)
            if eng == "D":
                nc.vector.tensor_copy(out=dst, in_=src)
            else:
                nc.scalar.copy(out=dst, in_=src)

        def yquant(b, lo, hi):
            nc.vector.quantize_mx(
                out=y_codes[:, b, lo:hi].bitcast(FP8X4), scales=y_scales[:, b, lo:hi],
                in_=grouped["y", b][:, lo:hi, :].rearrange("p c t -> p (c t)"))

        words_out = out_1[0].rearrange("p m t -> p (m t)").bitcast(I32)
        scales_out = out_2[0].bitcast(I32)

        def st_words(b, lo, hi):
            nc.sync.dma_start(out=words_out[:, b * C + lo:b * C + hi], in_=y_codes[:, b, lo:hi].bitcast(I32))

        def st_scales(engines):
            for Q in range(4):
                engines[Q % len(engines)].dma_start(
                    out=scales_out[4 * Q:4 * Q + 4, :],
                    in_=y_scales[32 * Q:32 * Q + 4, :, :].rearrange("p b c -> p (b c)").bitcast(I32))

        def warm_root():
            nc.scalar.activation(out=warm[:], in_=zero[:], func=ACT.Abs_reciprocal_sqrt, bias=eps[:])

        small = {}

        def spread_u():
            small["u"] = psum.tile([P, C], F32, name="acc")
            nc.tensor.matmul(small["u"][:], lhsT=ident_b[:, 0:1].to_broadcast([P, P]), rhs=rows[:], start=True, stop=True)

        def spread_temp():
            small["t"] = turn.tile([P, P], BF16, name="words")
            nc.tensor.transpose(small["t"][:], rows[:, 0:P], ident_b[:])

        def prep_temp():
            nc.vector.tensor_scalar(out=neg_temp[:], in0=small["t"][:, 1:1 + T], scalar1=-1.0 / math.sqrt(N), scalar2=None, op0=ALU.mult)

        def prep_u():
            nc.scalar.activation(
                out=u_perm[:].rearrange("p (h m e) -> p h m e", h=2, e=2),
                in_=small["u"][:].rearrange("p (m h e) -> p h m e", h=2, e=2), func=ACT.Copy, scale=math.sqrt(C))

        spread_temp()
        inter("D", "k", 0, 0, 352)
        inter("A", "k", 0, 352, 512)
        inter("D", "q", 0, 0, 256)
        inter("A", "q", 0, 256, 512)
        quant("k", 0, 0, 512)
        quant("q", 0, 0, 256)
        inter("D", "k", 1, 0, 256)
        inter("A", "k", 1, 256, 512)
        prep_temp()
        quant("q", 0, 256, 512)
        for i in range(T):
            g(0, i)
        spread_u()
        inter("A", "q", 1, 0, 256)
        rowmax(0, 0)
        quant("k", 1, 0, 512)
        rowmax(0, 1)
        inter("A", "q", 1, 256, 512)
        ex(0, 0)
        rowmax(0, 2)
        quant("q", 1, 0, 256)
        ex(0, 1)
        prep_u()
        rowmax(0, 3)
        quant("q", 1, 256, 512)
        for i in range(T):
            g(1, i)
        for t in range(T):
            tv(0, t)
        ex(0, 2)
        ex(0, 3)
        cp("v", 0, 0)
        rowmax(1, 0)
        rowmax(1, 1)
        rec(0, 0)
        rowmax(1, 2)
        ex(1, 0)
        cp("v", 0, 1)
        mulu(0, 0)
        tp(0, 0)
        mulu(0, 1)
        tp(0, 1)
        rec(0, 1)
        ex(1, 1)
        rowmax(1, 3)
        cp("p", 0, 0)
        mulu(0, 2)
        tp(0, 2)
        mulu(0, 3)
        tp(0, 3)
        ex(1, 2)
        ex(1, 3)
        cp("p", 0, 1)
        quant("v", 0, 0, 512)
        rec(1, 0)
        quant("p", 0, 0, 256)
        for t in range(T):
            tv(1, t)
        mulu(1, 0)
        tp(1, 0)
        rec(1, 1)
        mulu(1, 1)
        tp(1, 1)
        quant("p", 0, 256, 512)
        cp("v", 1, 0)
        cp("v", 1, 1)
        warm_root()
        for t in range(T):
            om(0, t)
        mulu(1, 2)
        tp(1, 2)
        mulu(1, 3)
        tp(1, 3)
        quant("v", 1, 0, 512)
        cp("p", 1, 0)
        sq(0, 0)
        modz(0, 0)
        modz(0, 1)
        cp("p", 1, 1)
        quant("p", 1, 0, 256)
        modz(0, 2)
        quant("p", 1, 256, 512)
        modz(0, 3)
        sq(0, 1)
        rs(0, 0)
        sq(0, 2)
        sq(0, 3)
        rs(0, 1)
        for t in range(T):
            om(1, t)
        fin(0, 0, 0, 512)
        fin(0, 1, 0, 512)
        st(0, 0, 2, 0, 512)
        modz(1, 0)
        fin(0, 2, 0, 512)
        fin(0, 3, 0, 512)
        st(0, 2, 4, 0, 512)
        for t in range(T):
            if t > 0:
                modz(1, t)
            sq(1, t)
            if t % 2:
                rs(1, t // 2)
        ycopy("A", 0, 0, 256)
        ycopy("A", 0, 256, 512)
        for t in range(T):
            fin(1, t, 0, 256)
        st(1, 0, T, 0, 256)
        ycopy("A", 1, 0, 128)
        ycopy("A", 1, 128, 256)
        for t in range(T):
            fin(1, t, 256, 512)
            if t == 1:
                yquant(0, 0, 512)
                st_words(0, 0, 512)
            if t % 2:
                st(1, t - 1, t + 1, 256, 512)
        ycopy("A", 1, 256, 352)
        yquant(1, 0, 256)
        st_words(1, 0, 256)
        ycopy("D", 1, 352, 512)
        yquant(1, 256, 512)
        st_words(1, 256, 512)
        st_scales([nc.scalar, nc.sync])
